import numpy as np
import ml_dtypes


def mxq(x, axis, fmt="e4m3"):
    dtype, down = {"e4m3": (ml_dtypes.float8_e4m3fn, 7), "e5m2": (ml_dtypes.float8_e5m2, 14)}[fmt]
    v = np.moveaxis(np.asarray(x, np.float32).astype(ml_dtypes.bfloat16).astype(np.float64), axis, -1)
    blocks = v.reshape(v.shape[:-1] + (-1, 32))
    amax = np.abs(blocks).max(-1, keepdims=True)
    byte = np.maximum(np.where(amax > 0, np.frexp(amax)[1] - 1 + 127, 0) - down, 1)
    scale = np.exp2(byte - 127.0)
    codes = (blocks / scale).astype(np.float32).astype(dtype).astype(np.float64)
    return np.moveaxis((codes * scale).reshape(v.shape), -1, axis)


WIDE = False


def mx_kscale(k):
    if not WIDE:
        return np.ones(k)
    levels = np.array([10, -10, 5, -5, 0])
    if k % 512:
        return np.exp2(np.random.permutation(np.resize(levels, k // 32))).repeat(32)
    a = np.empty((k // 512, 16))
    for p in range(k // 512):
        a[p, :8] = np.random.permutation(np.resize(levels, 8))
        for g in range(8):
            far = levels[np.abs(levels - a[p, g]) >= 10]
            a[p, g + 8] = far[np.random.randint(len(far))]
    return np.exp2(a.ravel()).repeat(32)


def f64(x):
    return np.asarray(x).astype(np.float64)


def striped(idx):
    return np.tile(idx.reshape(-1, 16).T, (8, 1)).astype(np.uint16)


def unstriped(offs):
    return offs[:16].T.reshape(-1).astype(np.int64)


E2M1 = np.array([0.0, 0.5, 1.0, 1.5, 2.0, 3.0, 4.0, 6.0, -0.0, -0.5, -1.0, -1.5, -2.0, -3.0, -4.0, -6.0])


def pack_weight(w, fmt):
    k, n = w.shape
    w = f64(np.asarray(w, np.float32).astype(ml_dtypes.bfloat16)).reshape(k // 32, 32, n)
    amax = np.abs(w).max(1)
    if fmt == "e4m3":
        byte = np.frexp(amax)[1] - 1 + 127 - 7
    else:
        mant, ex = np.frexp(amax / 6.0)
        byte = np.where(mant > 0.5, ex, ex - 1) + 127
    byte = np.clip(np.where(amax > 0, byte, 1), 1, 254)
    scaled = (w * np.exp2(127.0 - byte)[:, None, :]).reshape(k, n).astype(np.float32)
    by_word = np.ascontiguousarray(scaled.reshape(k // 512, 128, 4, n).transpose(0, 1, 3, 2))
    if fmt == "e4m3":
        words = by_word.astype(ml_dtypes.float8_e4m3fn).view(np.uint8)
    else:
        c = by_word.astype(ml_dtypes.float4_e2m1fn).view(np.uint8) & 0xF
        words = (c[..., 0::2] | (c[..., 1::2] << 4)).reshape(k // 512, 128, 2 * n)
    return np.ascontiguousarray(words), np.ascontiguousarray(byte.astype(np.uint8).reshape(k // 512, 16, n))


def unpack_weight(words, scales, fmt):
    g, _, n = scales.shape
    words = np.ascontiguousarray(words).reshape(g, 128, n, -1)
    if fmt == "e4m3":
        vals = words.view(ml_dtypes.float8_e4m3fn).astype(np.float64)
    else:
        nib = np.empty((g, 128, n, 4), np.uint8)
        nib[..., 0::2] = words & 0xF
        nib[..., 1::2] = words >> 4
        vals = E2M1[nib]
    vals = vals * np.repeat(np.exp2(scales.astype(np.float64) - 127.0), 8, axis=1)[..., None]
    return vals.transpose(0, 1, 3, 2).reshape(g * 512, n)


def gelu(v):
    return 0.5 * v * (1.0 + np.tanh(np.sqrt(2.0 / np.pi) * (v + 0.044715 * v**3)))


def twice(P):
    return np.random.permutation(np.repeat(np.arange(P), 2))


K, H, T, S, P = 1536, 1024, 2048, 1024, 512

def setup_inputs():
    n = np.random.standard_normal
    s = mx_kscale(K)[:, None]
    u = mx_kscale(H)[:, None]
    d = {}
    d["tab_words"], d["tab_scales"] = pack_weight(n((K, T)) * s, "e4m3")
    d["offs"] = striped(np.random.permutation(T)[:S])
    d["w1"] = (n((K, H)) / K**0.5 / s * u.T).astype(np.float32)
    d["b1"] = (0.5 * n(H) * u[:, 0]).astype(np.float32)
    d["pos1"] = striped(np.random.permutation(S)[:P])
    d["pos2"] = striped(np.random.permutation(S)[:P])
    d["pos3"] = striped(twice(P))
    d["w2_words"], d["w2_scales"] = pack_weight(1.4 * n((H, H)) / H**0.5 / u, "e2m1")
    d["gv"] = (0.8 * n(H) / u[:, 0]).astype(np.float32)
    d["hv"] = (np.exp(0.4 * n(H)) / u[:, 0]).astype(np.float32)
    return d

def reference(tab_words, tab_scales, offs, w1, b1, pos1, pos2, pos3, w2_words, w2_scales, gv, hv):
    v = unpack_weight(tab_words, tab_scales, "e4m3")[:, unstriped(offs)]
    w1q = mxq(f64(w1), 0, "e4m3")
    h = (w1q.T @ v) + f64(b1)[:, None]
    peak = np.maximum(h[:, unstriped(pos1)], h[:, unstriped(pos2)])
    peakq = mxq(peak, 0, "e4m3")
    w2 = unpack_weight(w2_words, w2_scales, "e2m1")
    y = np.tanh(w2.T @ peakq) + f64(gv)[:, None] * peak
    out = y[:, unstriped(pos3)] * (f64(hv)[:, None] * h)
    return out

@@ -1,0 +1,289 @@
+from contextlib import ExitStack
+
+import concourse.mybir as mybir
+from concourse.masks import make_identity
+
+K, H, T, S, R = 1536, 1024, 2048, 1024, 512
+FLOPS = 2 * K * H * S + 2 * H * H * R
+
+F32 = mybir.dt.float32
+BF16 = mybir.dt.bfloat16
+I32 = mybir.dt.int32
+U32 = mybir.dt.uint32
+U16 = mybir.dt.uint16
+U8 = mybir.dt.uint8
+FP8X4 = mybir.dt.float8_e4m3fn_x4
+FP4X4 = mybir.dt.float4_e2m1fn_x4
+ALU = mybir.AluOpType
+ACT = mybir.ActivationFunctionType
+
+P = 128
+PACK = 4
+K_PASS = P * PACK
+BANK = 512
+PASSES1 = K // K_PASS
+PASSES2 = H // K_PASS
+SLICES = H // P
+SLICES_PER_PASS = K_PASS // P
+BLOCKS = R // P
+W1_CHUNKS = (128, 128, 256, 256, 256)
+Y_WINDOW = R + 16
+TURN_LAG = 3
+HALF = R // 2
+
+
+def tile_list_graft_region_score_kernel(
+    tc, tab_words, tab_scales, offs, w1, b1, pos1, pos2, pos3, w2_words, w2_scales, gv, hv, out
+):
+    nc = tc.nc
+    with ExitStack() as ctx:
+        lists = ctx.enter_context(tc.tile_pool(name="lists", bufs=1))
+        keep = ctx.enter_context(tc.tile_pool(name="keep", bufs=1))
+        ring = ctx.enter_context(tc.tile_pool(name="ring", bufs=2))
+        psum = ctx.enter_context(tc.psum_pool(name="psum", bufs=1))
+        banks = [psum.tile([P, BANK], F32, name="bank%d" % i) for i in range(8)]
+
+        offs_sb = lists.tile([P, S // 16], U16, name="offs_sb")
+        pos1_sb = lists.tile([P, R // 16], U16, name="pos1_sb")
+        pos2_sb = lists.tile([P, R // 16], U16, name="pos2_sb")
+        pos3_sb = lists.tile([P, S // 16], U16, name="pos3_sb")
+
+        tab_sc = keep.tile([P, T], U8, name="tab_sc", tag="shared", align_bytes=64)
+        w2_sc = keep.tile([P, PASSES2, H], U8, name="w2_sc", align_bytes=64)
+        w2_sb = keep.tile([P, PASSES2, 2 * H], U8, name="w2_sb", align_bytes=64)
+        tab_sb = [keep.tile([P, T], I32, name="tab_sb%d" % a, align_bytes=64) for a in range(PASSES1)]
+        v_words = [keep.tile([P, S], U32, name="v_words%d" % a, align_bytes=64) for a in range(PASSES1 - 1)]
+        v_sc = keep.tile([P, S], U8, name="v_sc", align_bytes=64)
+        y_tiles = [keep.tile([P, Y_WINDOW], F32, name="y%d" % i, align_bytes=64) for i in range(SLICES)]
+        ident = keep.tile([P, P], F32, name="ident", align_bytes=64)
+        vec_rows = keep.tile([P, P], F32, name="vec_rows", align_bytes=64)
+        vec_cols = keep.tile([P, 3 * SLICES], F32, name="vec_cols", align_bytes=64)
+
+        nc.gpsimd.memset(tab_sc[:].bitcast(I32), 0)
+        for q in range(4):
+            nc.gpsimd.dma_start(
+                out=tab_sc[32 * q : 32 * q + 4 * PASSES1, :].bitcast(I32),
+                in_=tab_scales[:, 4 * q : 4 * q + 4, :].bitcast(I32),
+            )
+        nc.vector.memset(w2_sc[:].rearrange("p a n -> p (a n)").bitcast(I32), 0)
+        for y in y_tiles:
+            nc.vector.memset(y[:, R:], 0.0)
+
+        nc.vector.memset(vec_rows[:], 0.0)
+        for i, vec in enumerate((b1, gv, hv)):
+            nc.gpsimd.dma_start(
+                out=vec_rows[i * SLICES : (i + 1) * SLICES, :], in_=vec.rearrange("(c p) -> c p", p=P)
+            )
+        make_identity(nc, ident[:])
+        nc.tensor.transpose(banks[7][:, 0:P], vec_rows[:], ident[:])
+        nc.scalar.copy(out=vec_cols[:], in_=banks[7][:, 0 : 3 * SLICES])
+
+        def load_table(a):
+            nc.sync.dma_start(out=tab_sb[a][:], in_=tab_words[a].rearrange("p t i -> p (t i)").bitcast(I32))
+
+        def gather_table(a, lo, hi):
+            nc.vector.tensor_copy(
+                out=v_words[a][:, lo:hi], in_=tab_sb[a][:].bitcast(U32).indirect(offs_sb[:, lo // 16 : hi // 16])
+            )
+
+        w1_codes = {}
+        w1_scales = {}
+        stages = {}
+
+        def load_w1(chunk):
+            c0 = sum(W1_CHUNKS[:chunk])
+            width = W1_CHUNKS[chunk]
+            raws = []
+            for a in range(PASSES1):
+                raw = keep.tile([P, PACK * width], F32, name="raw%d_%d" % (chunk, a), align_bytes=64)
+                rows = w1[a * K_PASS : (a + 1) * K_PASS, c0 : c0 + width]
+                nc.sync.dma_start(out=raw[:].rearrange("p (j c) -> p j c", j=PACK), in_=rows.rearrange("(p j) c -> p j c", j=PACK))
+                raws.append(raw)
+            return raws
+
+        def quantise_w1(chunk, raws):
+            c0 = sum(W1_CHUNKS[:chunk])
+            width = W1_CHUNKS[chunk]
+            for a in range(PASSES1):
+                stage = keep.tile([P, 2 * width], F32, name="stage%d_%d" % (chunk, a), align_bytes=64)
+                stages[(chunk, a)] = stage
+                grouped = stage[:].bitcast(BF16)
+                nc.scalar.copy(
+                    out=grouped.rearrange("p (c i j) -> p c j i", i=4, j=PACK),
+                    in_=raws[a][:].rearrange("p (j c i) -> p c j i", i=4, j=PACK),
+                )
+                codes = keep.tile([P, width], U32, name="w1_codes%d_%d" % (chunk, a), align_bytes=64)
+                scales = keep.tile([P, width], U8, name="w1_scales%d_%d" % (chunk, a), align_bytes=64)
+                nc.vector.quantize_mx(
+                    out=codes[:].bitcast(FP8X4), scales=scales[:], in_=grouped
+                )
+                for off in range(0, width, P):
+                    w1_codes[((c0 + off) // P, a)] = codes[:, off : off + P]
+                    w1_scales[((c0 + off) // P, a)] = scales[:, off : off + P]
+
+        nc.sync.dma_start(offs_sb[:], offs)
+        load_table(0)
+        load_table(1)
+        raws = {0: load_w1(0)}
+        load_table(2)
+        raws[1] = load_w1(1)
+        nc.sync.dma_start(pos1_sb[:], pos1)
+        nc.sync.dma_start(pos2_sb[:], pos2)
+        for chunk in range(2, len(W1_CHUNKS)):
+            raws[chunk] = load_w1(chunk)
+        nc.sync.dma_start(
+            out=w2_sb[:].bitcast(I32), in_=w2_words.bitcast(I32).rearrange("a p n -> p a n")
+        )
+        nc.sync.dma_start(pos3_sb[:], pos3)
+        for q in range(4):
+            nc.sync.dma_start(
+                out=w2_sc[32 * q : 32 * q + 4, :, :].bitcast(I32),
+                in_=w2_scales[:, 4 * q : 4 * q + 4, :].bitcast(I32).rearrange("a r n -> r a n"),
+            )
+
+        gather_table(0, 0, S)
+        nc.vector.tensor_copy(out=v_sc[:], in_=tab_sc[:].indirect(offs_sb[:]))
+        gather_table(1, 0, S)
+        quantise_w1(0, raws[0])
+        v_words.append(keep.tile([P, S], U32, name="v_words2", tag="shared", align_bytes=64))
+        gather_table(2, 0, BANK)
+        gather_table(2, BANK, S)
+        quantise_w1(1, raws[1])
+
+        spare = [keep.tile([P, R], F32, name="spare%d" % i, align_bytes=64) for i in range(2)]
+        h_tiles = []
+        peaks = []
+        peak_codes = []
+        peak_scales = []
+        turned = [
+            keep.tile([P, BLOCKS, 2, 2 * P], BF16, name="turned%d" % b, align_bytes=64) for b in range(PASSES2)
+        ]
+        stage_chunk = (None, 2, 3, None, 4, 2, 3, None)
+
+        def features(c):
+            h = keep.tile([P, S], F32, name="h%d" % c, align_bytes=64)
+            accs = banks[2 * (c % 2) : 2 * (c % 2) + 2]
+            for a in range(PASSES1):
+                for half in range(2):
+                    cols = slice(half * BANK, (half + 1) * BANK)
+                    nc.tensor.matmul_mx(
+                        out=accs[half][:],
+                        lhsT=w1_codes[(c, a)].bitcast(FP8X4),
+                        lhsT_scale=w1_scales[(c, a)],
+                        rhs=v_words[a][:, cols].bitcast(FP8X4),
+                        rhs_scale=v_sc[4 * a : P, cols],
+                        start=(a == 0),
+                        stop=(a == PASSES1 - 1),
+                    )
+            for half in range(2):
+                nc.scalar.activation(
+                    out=h[:, half * BANK : (half + 1) * BANK],
+                    in_=accs[half][:],
+                    func=ACT.Identity,
+                    bias=vec_cols[:, c : c + 1],
+                    scale=1.0,
+                )
+            h_tiles.append(h)
+
+        def maxima(c):
+            h = h_tiles[c]
+            chunk = stage_chunk[c]
+            first, second = spare if chunk is None else (stages[(chunk, 2)], stages[(chunk, 1)])
+            peak = keep.tile([P, R], F32, name="peak%d" % c, align_bytes=64)
+            nc.vector.tensor_copy(out=first[:], in_=h[:].indirect(pos1_sb[:]))
+            for lo in range(0, R, HALF):
+                nc.vector.tensor_copy(
+                    out=second[:, lo : lo + HALF], in_=h[:].indirect(pos2_sb[:, lo // 16 : (lo + HALF) // 16])
+                )
+            for lo in range(0, R, HALF):
+                cols = slice(lo, lo + HALF)
+                nc.vector.tensor_tensor(out=peak[:, cols], in0=first[:, cols], in1=second[:, cols], op=ALU.max)
+            peaks.append(peak)
+
+        def turn(c):
+            b, quad = divmod(c, SLICES_PER_PASS)
+            bank = banks[2 * ((c + TURN_LAG) % 2)]
+            for j in range(BLOCKS):
+                nc.tensor.transpose(bank[:, j * P : (j + 1) * P], peaks[c][:, j * P : (j + 1) * P], ident[:])
+            nc.scalar.copy(
+                out=turned[b][:, :, :, 64 * quad : 64 * (quad + 1)].rearrange("p j u (q e) -> p u j q e", e=2),
+                in_=bank[:].rearrange("p (j q u e) -> p u j q e", j=BLOCKS, u=2, e=2),
+            )
+
+        def quantise_peak(b):
+            words = turned[b][:].bitcast(F32)
+            grouped = keep.tile([P, R * PACK], BF16, name="peak_grouped%d" % b, align_bytes=64)
+            grouped_words = grouped[:].bitcast(F32).rearrange("p (j m u) -> p j m u", m=P, u=2)
+            for j0 in range(0, BLOCKS, 2):
+                bank = banks[4 + j0 // 2][:].rearrange("p (j u m) -> p j u m", u=2, m=P)
+                for j in range(2):
+                    for u in range(2):
+                        nc.tensor.transpose(bank[:, j, u, :], words[:, j0 + j, u, :], ident[:])
+                nc.scalar.copy(out=grouped_words[:, j0 : j0 + 2, :, :], in_=bank.rearrange("p j u m -> p j m u"))
+            codes = keep.tile([P, R], U32, name="peak_codes%d" % b, align_bytes=64)
+            scales = keep.tile([P, R], U8, name="peak_scales%d" % b, align_bytes=64)
+            nc.vector.quantize_mx(out=codes[:].bitcast(FP8X4), scales=scales[:], in_=grouped[:])
+            peak_codes.append(codes)
+            peak_scales.append(scales)
+
+        for step in range(SLICES + TURN_LAG):
+            if step < SLICES:
+                features(step)
+                if step in (0, 1, 3):
+                    quantise_w1(2 + (step + 1) // 2, raws[2 + (step + 1) // 2])
+                maxima(step)
+            if step >= TURN_LAG:
+                turn(step - TURN_LAG)
+                if (step - TURN_LAG) % SLICES_PER_PASS == SLICES_PER_PASS - 1:
+                    quantise_peak((step - TURN_LAG) // SLICES_PER_PASS)
+
+        def scores(c):
+            acc = banks[(6 + c) % 8]
+            for b in range(PASSES2):
+                nc.tensor.matmul_mx(
+                    out=acc[:],
+                    lhsT=w2_sb[:, b, 2 * P * c : 2 * P * (c + 1)].bitcast(FP4X4),
+                    lhsT_scale=w2_sc[:, b, P * c : P * (c + 1)],
+                    rhs=peak_codes[b][:].bitcast(FP8X4),
+                    rhs_scale=peak_scales[b][:],
+                    start=(b == 0),
+                    stop=(b == PASSES2 - 1),
+                )
+            bounded = ring.tile([P, R], F32, name="bounded", tag="bounded", bufs=3, align_bytes=64)
+            nc.scalar.activation(out=bounded[:], in_=acc[:], func=ACT.Tanh)
+            nc.vector.scalar_tensor_tensor(
+                out=y_tiles[c][:, 0:R],
+                in0=peaks[c][:],
+                scalar=vec_cols[:, SLICES + c : SLICES + c + 1],
+                in1=bounded[:],
+                op0=ALU.mult,
+                op1=ALU.add,
+            )
+
+        def finish(c):
+            scaled = raws[4][c % PASSES1]
+            nc.scalar.activation(
+                out=scaled[:],
+                in_=h_tiles[c][:],
+                func=ACT.Copy,
+                scale=vec_cols[:, 2 * SLICES + c : 2 * SLICES + c + 1],
+            )
+            result = (raws[2] + raws[3])[c % (2 * PASSES1)]
+            width = BANK // 2 if c == SLICES - 1 else BANK
+            for lo in range(0, S, width):
+                nc.vector.tensor_tensor(
+                    out=result[:, lo : lo + width],
+                    in0=y_tiles[c][:].indirect(pos3_sb[:, lo // 16 : (lo + width) // 16]),
+                    in1=scaled[:, lo : lo + width],
+                    op=ALU.mult,
+                )
+                if c == SLICES - 1:
+                    nc.sync.dma_start(out=out[c * P : (c + 1) * P, lo : lo + width], in_=result[:, lo : lo + width])
+            if c < SLICES - 1:
+                nc.sync.dma_start(out=out[c * P : (c + 1) * P, :], in_=result[:])
+
+        scores(0)
+        for c in range(SLICES):
+            if c + 1 < SLICES:
+                scores(c + 1)
+            finish(c)

@@ -26,7 +26,7 @@ PASSES2 = H // K_PASS
 SLICES = H // P
 SLICES_PER_PASS = K_PASS // P
 BLOCKS = R // P
-W1_CHUNKS = (128, 128, 256, 256, 256)
+W1_CHUNKS = (128, 128, 256, 512)
 Y_WINDOW = R + 16
 TURN_LAG = 3
 HALF = R // 2
@@ -50,33 +50,32 @@ def tile_list_graft_region_score_kernel(
 
         tab_sc = keep.tile([P, T], U8, name="tab_sc", tag="shared", align_bytes=64)
         w2_sc = keep.tile([P, PASSES2, H], U8, name="w2_sc", align_bytes=64)
-        w2_sb = keep.tile([P, PASSES2, 2 * H], U8, name="w2_sb", align_bytes=64)
+        w2_low = keep.tile([P, PASSES2, 2 * K_PASS], U8, name="w2_low", align_bytes=64)
+        w2_high = keep.tile([P, PASSES2, 2 * K_PASS], U8, name="w2_high", align_bytes=64)
+        w2_dealt = keep.tile([P, PASSES2, 2 * K_PASS], U8, name="w2_dealt", align_bytes=64)
+        w2_sc_dealt = keep.tile([P, PASSES2, K_PASS], U8, name="w2_sc_dealt", align_bytes=64)
+        high_cols = [keep.tile([P, PACK], F32, name="high_cols%d" % i, align_bytes=64) for i in range(3)]
         tab_sb = [keep.tile([P, T], I32, name="tab_sb%d" % a, align_bytes=64) for a in range(PASSES1)]
         v_words = [keep.tile([P, S], U32, name="v_words%d" % a, align_bytes=64) for a in range(PASSES1 - 1)]
         v_sc = keep.tile([P, S], U8, name="v_sc", align_bytes=64)
         y_tiles = [keep.tile([P, Y_WINDOW], F32, name="y%d" % i, align_bytes=64) for i in range(SLICES)]
         ident = keep.tile([P, P], F32, name="ident", align_bytes=64)
         vec_rows = keep.tile([P, P], F32, name="vec_rows", align_bytes=64)
-        vec_cols = keep.tile([P, 3 * SLICES], F32, name="vec_cols", align_bytes=64)
+        vec_cols = keep.tile([P, 3 * PACK], F32, name="vec_cols", align_bytes=64)
 
-        nc.gpsimd.memset(tab_sc[:].bitcast(I32), 0)
+        sc_rows = keep.tile([P, T // 4], I32, name="sc_rows", align_bytes=64)
         for q in range(4):
-            nc.gpsimd.dma_start(
-                out=tab_sc[32 * q : 32 * q + 4 * PASSES1, :].bitcast(I32),
+            nc.scalar.dma_start(
+                out=sc_rows[32 * q : 32 * q + 4 * PASSES1, :],
                 in_=tab_scales[:, 4 * q : 4 * q + 4, :].bitcast(I32),
             )
+        nc.vector.memset(tab_sc[:].bitcast(I32), 0)
         nc.vector.memset(w2_sc[:].rearrange("p a n -> p (a n)").bitcast(I32), 0)
         for y in y_tiles:
             nc.vector.memset(y[:, R:], 0.0)
 
         nc.vector.memset(vec_rows[:], 0.0)
-        for i, vec in enumerate((b1, gv, hv)):
-            nc.gpsimd.dma_start(
-                out=vec_rows[i * SLICES : (i + 1) * SLICES, :], in_=vec.rearrange("(c p) -> c p", p=P)
-            )
         make_identity(nc, ident[:])
-        nc.tensor.transpose(banks[7][:, 0:P], vec_rows[:], ident[:])
-        nc.scalar.copy(out=vec_cols[:], in_=banks[7][:, 0 : 3 * SLICES])
 
         def load_table(a):
             nc.sync.dma_start(out=tab_sb[a][:], in_=tab_words[a].rearrange("p t i -> p (t i)").bitcast(I32))
@@ -95,7 +94,7 @@ def tile_list_graft_region_score_kernel(
             width = W1_CHUNKS[chunk]
             raws = []
             for a in range(PASSES1):
-                raw = keep.tile([P, PACK * width], F32, name="raw%d_%d" % (chunk, a), align_bytes=64)
+                raw = keep.tile([P, PACK * width], F32, name="raw%d_%d" % (chunk, a), tag="raw%d_%d" % (chunk, a), align_bytes=64)
                 rows = w1[a * K_PASS : (a + 1) * K_PASS, c0 : c0 + width]
                 nc.sync.dma_start(out=raw[:].rearrange("p (j c) -> p j c", j=PACK), in_=rows.rearrange("(p j) c -> p j c", j=PACK))
                 raws.append(raw)
@@ -108,8 +107,9 @@ def tile_list_graft_region_score_kernel(
                 stage = keep.tile([P, 2 * width], F32, name="stage%d_%d" % (chunk, a), align_bytes=64)
                 stages[(chunk, a)] = stage
                 grouped = stage[:].bitcast(BF16)
+                order = "p (i c j) -> p c j i" if width == K_PASS else "p (c i j) -> p c j i"
                 nc.scalar.copy(
-                    out=grouped.rearrange("p (c i j) -> p c j i", i=4, j=PACK),
+                    out=grouped.rearrange(order, i=4, j=PACK),
                     in_=raws[a][:].rearrange("p (j c i) -> p c j i", i=4, j=PACK),
                 )
                 codes = keep.tile([P, width], U32, name="w1_codes%d_%d" % (chunk, a), align_bytes=64)
@@ -123,31 +123,55 @@ def tile_list_graft_region_score_kernel(
 
         nc.sync.dma_start(offs_sb[:], offs)
         load_table(0)
-        load_table(1)
+        for i, vec in enumerate((b1, gv, hv)):
+            nc.sync.dma_start(
+                out=vec_rows[i * PACK : (i + 1) * PACK, :], in_=vec[0:K_PASS].rearrange("(c p) -> c p", p=P)
+            )
         raws = {0: load_w1(0)}
+        load_table(1)
         load_table(2)
-        raws[1] = load_w1(1)
-        nc.sync.dma_start(pos1_sb[:], pos1)
-        nc.sync.dma_start(pos2_sb[:], pos2)
-        for chunk in range(2, len(W1_CHUNKS)):
-            raws[chunk] = load_w1(chunk)
-        nc.sync.dma_start(
-            out=w2_sb[:].bitcast(I32), in_=w2_words.bitcast(I32).rearrange("a p n -> p a n")
-        )
-        nc.sync.dma_start(pos3_sb[:], pos3)
+        w2_rows = w2_words.bitcast(I32).rearrange("a p n -> p a n")
+        nc.sync.dma_start(out=w2_high[:].bitcast(I32), in_=w2_rows[:, :, K_PASS // 2 : K_PASS])
         for q in range(4):
             nc.sync.dma_start(
                 out=w2_sc[32 * q : 32 * q + 4, :, :].bitcast(I32),
                 in_=w2_scales[:, 4 * q : 4 * q + 4, :].bitcast(I32).rearrange("a r n -> r a n"),
             )
+        raws[1] = load_w1(1)
+        nc.sync.dma_start(pos1_sb[:], pos1)
+        nc.sync.dma_start(pos2_sb[:], pos2)
+        raws[2] = load_w1(2)
+        raws[3] = load_w1(3)
+        for i, vec in enumerate((b1, gv, hv)):
+            nc.sync.dma_start(out=high_cols[i][:], in_=vec[K_PASS:H].rearrange("(p t) -> p t", t=PACK))
+        nc.sync.dma_start(out=w2_low[:].bitcast(I32), in_=w2_rows[:, :, 0 : K_PASS // 2])
+        nc.sync.dma_start(pos3_sb[:], pos3)
 
+        def column(i, c):
+            if c < PACK:
+                return vec_cols[:, i * PACK + c : i * PACK + c + 1]
+            return high_cols[i][:, c - PACK : c - PACK + 1]
+
+        for q in range(4):
+            rows = slice(32 * q, 32 * q + 4 * PASSES1)
+            nc.vector.tensor_copy(out=tab_sc[rows, :].bitcast(I32), in_=sc_rows[rows, :])
+        nc.tensor.transpose(banks[7][:, 0:P], vec_rows[:], ident[:])
+        nc.scalar.activation(out=vec_cols[:], in_=banks[7][:, 0 : 3 * PACK], func=ACT.Identity)
         gather_table(0, 0, S)
         nc.vector.tensor_copy(out=v_sc[:], in_=tab_sc[:].indirect(offs_sb[:]))
-        gather_table(1, 0, S)
         quantise_w1(0, raws[0])
+        gather_table(1, 0, S)
         v_words.append(keep.tile([P, S], U32, name="v_words2", tag="shared", align_bytes=64))
         gather_table(2, 0, BANK)
         gather_table(2, BANK, S)
+        nc.vector.tensor_copy(
+            out=w2_dealt[:].bitcast(U16).rearrange("p a (t q) -> p a t q", t=PACK),
+            in_=w2_high[:].bitcast(U16).rearrange("p a (q t) -> p a t q", t=PACK),
+        )
+        nc.vector.tensor_copy(
+            out=w2_sc_dealt[:].rearrange("p a (t q) -> p a t q", t=PACK),
+            in_=w2_sc[:, :, K_PASS:H].rearrange("p a (q t) -> p a t q", t=PACK),
+        )
         quantise_w1(1, raws[1])
 
         spare = [keep.tile([P, R], F32, name="spare%d" % i, align_bytes=64) for i in range(2)]
@@ -155,13 +179,19 @@ def tile_list_graft_region_score_kernel(
         peaks = []
         peak_codes = []
         peak_scales = []
-        turned = [
-            keep.tile([P, BLOCKS, 2, 2 * P], BF16, name="turned%d" % b, align_bytes=64) for b in range(PASSES2)
-        ]
-        stage_chunk = (None, 2, 3, None, 4, 2, 3, None)
+        turned = keep.tile([P, BLOCKS, 2, 2 * P], BF16, name="turned", align_bytes=64)
+        for b in range(PASSES2):
+            peak_codes.append(keep.tile([P, R], U32, name="peak_codes%d" % b, align_bytes=64))
+            peak_scales.append(keep.tile([P, R], U8, name="peak_scales%d" % b, align_bytes=64))
+        for c in range(PACK):
+            peaks.append(keep.tile([P, R], F32, name="peak%d" % c, align_bytes=64)[:])
+        peak_high = keep.tile([P, PACK, R], F32, name="peak_high", align_bytes=64)
+        for t in range(PACK):
+            peaks.append(peak_high[:, t, :])
 
         def features(c):
-            h = keep.tile([P, S], F32, name="h%d" % c, align_bytes=64)
+            tag = "raw3_%d" % (c - 1) if c in (2, 3) else "h%d" % c
+            h = keep.tile([P, S], F32, name="h%d" % c, tag=tag, align_bytes=64)
             accs = banks[2 * (c % 2) : 2 * (c % 2) + 2]
             for a in range(PASSES1):
                 for half in range(2):
@@ -180,39 +210,42 @@ def tile_list_graft_region_score_kernel(
                     out=h[:, half * BANK : (half + 1) * BANK],
                     in_=accs[half][:],
                     func=ACT.Identity,
-                    bias=vec_cols[:, c : c + 1],
+                    bias=column(0, c),
                     scale=1.0,
                 )
             h_tiles.append(h)
 
-        def maxima(c):
-            h = h_tiles[c]
-            chunk = stage_chunk[c]
-            first, second = spare if chunk is None else (stages[(chunk, 2)], stages[(chunk, 1)])
-            peak = keep.tile([P, R], F32, name="peak%d" % c, align_bytes=64)
-            nc.vector.tensor_copy(out=first[:], in_=h[:].indirect(pos1_sb[:]))
-            for lo in range(0, R, HALF):
-                nc.vector.tensor_copy(
-                    out=second[:, lo : lo + HALF], in_=h[:].indirect(pos2_sb[:, lo // 16 : (lo + HALF) // 16])
-                )
-            for lo in range(0, R, HALF):
-                cols = slice(lo, lo + HALF)
-                nc.vector.tensor_tensor(out=peak[:, cols], in0=first[:, cols], in1=second[:, cols], op=ALU.max)
-            peaks.append(peak)
+        def pick(c, positions, dst, lo, hi):
+            nc.vector.tensor_copy(out=dst, in_=h_tiles[c][:].indirect(positions[:, lo // 16 : hi // 16]))
 
-        def turn(c):
-            b, quad = divmod(c, SLICES_PER_PASS)
-            bank = banks[2 * ((c + TURN_LAG) % 2)]
+        def staging(c):
+            if c in (0, 4):
+                return spare[0][:], spare[1][:]
+            if c == 1:
+                return stages[(2, 2)][:], stages[(2, 1)][:]
+            stage = stages[(3, {2: 0, 3: 2, 5: 1, 6: 2, 7: 0}[c])]
+            return stage[:, 0:R], stage[:, R : 2 * R]
+
+        def maxima(c):
+            first, second = staging(c)
+            halves = (slice(0, HALF), slice(HALF, R))
+            pick(c, pos1_sb, first, 0, R)
+            for cols in halves:
+                pick(c, pos2_sb, second[:, cols], cols.start, cols.stop)
+            for cols in halves:
+                nc.vector.tensor_tensor(out=peaks[c][:, cols], in0=first[:, cols], in1=second[:, cols], op=ALU.max)
+
+        def turn(c, bank):
             for j in range(BLOCKS):
                 nc.tensor.transpose(bank[:, j * P : (j + 1) * P], peaks[c][:, j * P : (j + 1) * P], ident[:])
             nc.scalar.copy(
-                out=turned[b][:, :, :, 64 * quad : 64 * (quad + 1)].rearrange("p j u (q e) -> p u j q e", e=2),
+                out=turned[:, :, :, 64 * c : 64 * (c + 1)].rearrange("p j u (q e) -> p u j q e", e=2),
                 in_=bank[:].rearrange("p (j q u e) -> p u j q e", j=BLOCKS, u=2, e=2),
             )
 
-        def quantise_peak(b):
-            words = turned[b][:].bitcast(F32)
-            grouped = keep.tile([P, R * PACK], BF16, name="peak_grouped%d" % b, align_bytes=64)
+        def quantise_low_peak():
+            words = turned[:].bitcast(F32)
+            grouped = keep.tile([P, R * PACK], BF16, name="low_grouped", align_bytes=64)
             grouped_words = grouped[:].bitcast(F32).rearrange("p (j m u) -> p j m u", m=P, u=2)
             for j0 in range(0, BLOCKS, 2):
                 bank = banks[4 + j0 // 2][:].rearrange("p (j u m) -> p j u m", u=2, m=P)
@@ -220,55 +253,81 @@ def tile_list_graft_region_score_kernel(
                     for u in range(2):
                         nc.tensor.transpose(bank[:, j, u, :], words[:, j0 + j, u, :], ident[:])
                 nc.scalar.copy(out=grouped_words[:, j0 : j0 + 2, :, :], in_=bank.rearrange("p j u m -> p j m u"))
-            codes = keep.tile([P, R], U32, name="peak_codes%d" % b, align_bytes=64)
-            scales = keep.tile([P, R], U8, name="peak_scales%d" % b, align_bytes=64)
-            nc.vector.quantize_mx(out=codes[:].bitcast(FP8X4), scales=scales[:], in_=grouped[:])
-            peak_codes.append(codes)
-            peak_scales.append(scales)
+            nc.vector.quantize_mx(out=peak_codes[0][:].bitcast(FP8X4), scales=peak_scales[0][:], in_=grouped[:])
 
-        for step in range(SLICES + TURN_LAG):
-            if step < SLICES:
-                features(step)
-                if step in (0, 1, 3):
-                    quantise_w1(2 + (step + 1) // 2, raws[2 + (step + 1) // 2])
-                maxima(step)
-            if step >= TURN_LAG:
-                turn(step - TURN_LAG)
-                if (step - TURN_LAG) % SLICES_PER_PASS == SLICES_PER_PASS - 1:
-                    quantise_peak((step - TURN_LAG) // SLICES_PER_PASS)
+        def quantise_high_peak():
+            grouped = [
+                keep.tile([P, HALF * PACK], BF16, name="high_grouped%d" % i, align_bytes=64) for i in range(2)
+            ]
+            for i, copy in enumerate((nc.scalar.copy, nc.vector.tensor_copy)):
+                copy(
+                    out=grouped[i][:].rearrange("p (c i t) -> p c t i", i=4, t=PACK),
+                    in_=peak_high[:, :, i * HALF : (i + 1) * HALF].rearrange("p t (c i) -> p c t i", i=4),
+                )
+            for i in (1, 0):
+                cols = slice(i * HALF, (i + 1) * HALF)
+                nc.vector.quantize_mx(
+                    out=peak_codes[1][:, cols].bitcast(FP8X4), scales=peak_scales[1][:, cols], in_=grouped[i][:]
+                )
+
+        def scale_features(c):
+            nc.scalar.activation(
+                out=stages[(3, (c + 1) % PASSES1)][:],
+                in_=h_tiles[c][:],
+                func=ACT.Copy,
+                scale=column(2, c),
+            )
+
+        for step in range(SLICES):
+            features(step)
+            if step < 2:
+                quantise_w1(2 + step, raws[2 + step])
+            maxima(step)
+            c = step - TURN_LAG
+            if 0 <= c < PACK:
+                turn(c, banks[2 * (step % 2)])
+            if c == PACK - 1:
+                quantise_low_peak()
+        quantise_high_peak()
+        for early in range(PASSES1):
+            scale_features(early)
 
         def scores(c):
             acc = banks[(6 + c) % 8]
+            words, scales = (w2_low, w2_sc) if c < PACK else (w2_dealt, w2_sc_dealt)
+            n = c % PACK
             for b in range(PASSES2):
                 nc.tensor.matmul_mx(
                     out=acc[:],
-                    lhsT=w2_sb[:, b, 2 * P * c : 2 * P * (c + 1)].bitcast(FP4X4),
-                    lhsT_scale=w2_sc[:, b, P * c : P * (c + 1)],
+                    lhsT=words[:, b, 2 * P * n : 2 * P * (n + 1)].bitcast(FP4X4),
+                    lhsT_scale=scales[:, b, P * n : P * (n + 1)],
                     rhs=peak_codes[b][:].bitcast(FP8X4),
                     rhs_scale=peak_scales[b][:],
                     start=(b == 0),
                     stop=(b == PASSES2 - 1),
                 )
             bounded = ring.tile([P, R], F32, name="bounded", tag="bounded", bufs=3, align_bytes=64)
-            nc.scalar.activation(out=bounded[:], in_=acc[:], func=ACT.Tanh)
-            nc.vector.scalar_tensor_tensor(
-                out=y_tiles[c][:, 0:R],
-                in0=peaks[c][:],
-                scalar=vec_cols[:, SLICES + c : SLICES + c + 1],
-                in1=bounded[:],
-                op0=ALU.mult,
-                op1=ALU.add,
-            )
+            width = R // 2 if c == 0 else R
+            for lo in range(0, R, width):
+                cols = slice(lo, lo + width)
+                nc.scalar.activation(out=bounded[:, cols], in_=acc[:, cols], func=ACT.Tanh)
+                nc.vector.scalar_tensor_tensor(
+                    out=y_tiles[c][:, cols],
+                    in0=peaks[c][:, cols],
+                    scalar=column(1, c),
+                    in1=bounded[:, cols],
+                    op0=ALU.mult,
+                    op1=ALU.add,
+                )
+
+        results = [raw[:] for raw in raws[2]] + [raws[3][0][:, 0:S], raws[3][0][:, S : 2 * S]]
 
         def finish(c):
-            scaled = raws[4][c % PASSES1]
-            nc.scalar.activation(
-                out=scaled[:],
-                in_=h_tiles[c][:],
-                func=ACT.Copy,
-                scale=vec_cols[:, 2 * SLICES + c : 2 * SLICES + c + 1],
-            )
-            result = (raws[2] + raws[3])[c % (2 * PASSES1)]
+            scaled = stages[(3, (c + 1) % PASSES1)]
+            if c >= PASSES1:
+                scale_features(c)
+            result = results[c % len(results)]
+            rows = out[c * P : (c + 1) * P, :] if c < PACK else out[K_PASS:H, :].rearrange("(p t) s -> p t s", t=PACK)[:, c - PACK, :]
             width = BANK // 2 if c == SLICES - 1 else BANK
             for lo in range(0, S, width):
                 nc.vector.tensor_tensor(
@@ -278,9 +337,9 @@ def tile_list_graft_region_score_kernel(
                     op=ALU.mult,
                 )
                 if c == SLICES - 1:
-                    nc.sync.dma_start(out=out[c * P : (c + 1) * P, lo : lo + width], in_=result[:, lo : lo + width])
+                    nc.sync.dma_start(out=rows[:, lo : lo + width], in_=result[:, lo : lo + width])
             if c < SLICES - 1:
-                nc.sync.dma_start(out=out[c * P : (c + 1) * P, :], in_=result[:])
+                nc.sync.dma_start(out=rows, in_=result)
 
         scores(0)
         for c in range(SLICES):

@@ -30,6 +30,7 @@ W1_CHUNKS = (128, 128, 256, 512)
 Y_WINDOW = R + 16
 TURN_LAG = 3
 HALF = R // 2
+DIRECT = 2
 
 
 def tile_list_graft_region_score_kernel(
@@ -289,11 +290,33 @@ def tile_list_graft_region_score_kernel(
             if c == PACK - 1:
                 quantise_low_peak()
         quantise_high_peak()
-        for early in range(PASSES1):
-            scale_features(early)
+        for c in range(DIRECT):
+            scale_features(c)
+        weighted_tiles = [tile[:] for tile in spare] + [stages[(2, a)][:] for a in range(PASSES1)]
+        weighted_tiles.append(stages[(3, 0)][:, 0:R])
+
+        def add_by_transposes(c, bounded):
+            weighted = weighted_tiles[c - DIRECT]
+            nc.scalar.activation(out=weighted, in_=peaks[c], func=ACT.Copy, scale=column(1, c))
+            sums = banks[c % 2]
+            back = banks[2 + c % 2]
+            for j in range(BLOCKS):
+                cols = slice(j * P, (j + 1) * P)
+                nc.tensor.matmul(
+                    out=sums[:, cols], lhsT=weighted[:, cols], rhs=ident[:], is_transpose=True, start=True, stop=False
+                )
+                nc.tensor.matmul(
+                    out=sums[:, cols], lhsT=bounded[:, cols], rhs=ident[:], is_transpose=True, start=False, stop=True
+                )
+            summed = ring.tile([P, R], F32, name="summed", tag="summed", align_bytes=64)
+            nc.scalar.copy(out=summed[:], in_=sums[:])
+            for j in range(BLOCKS):
+                cols = slice(j * P, (j + 1) * P)
+                nc.tensor.transpose(back[:, cols], summed[:, cols], ident[:])
+            nc.scalar.activation(out=y_tiles[c][:, 0:R], in_=back[:], func=ACT.Copy, scale=column(2, c))
 
         def scores(c):
-            acc = banks[(6 + c) % 8]
+            acc = banks[4 + (c + 2) % 4]
             words, scales = (w2_low, w2_sc) if c < PACK else (w2_dealt, w2_sc_dealt)
             n = c % PACK
             for b in range(PASSES2):
@@ -307,6 +330,10 @@ def tile_list_graft_region_score_kernel(
                     stop=(b == PASSES2 - 1),
                 )
             bounded = ring.tile([P, R], F32, name="bounded", tag="bounded", bufs=3, align_bytes=64)
+            if c >= DIRECT:
+                nc.scalar.activation(out=bounded[:], in_=acc[:], func=ACT.Tanh)
+                add_by_transposes(c, bounded)
+                return
             width = R // 2 if c == 0 else R
             for lo in range(0, R, width):
                 cols = slice(lo, lo + width)
@@ -323,9 +350,7 @@ def tile_list_graft_region_score_kernel(
         results = [raw[:] for raw in raws[2]] + [raws[3][0][:, 0:S], raws[3][0][:, S : 2 * S]]
 
         def finish(c):
-            scaled = stages[(3, (c + 1) % PASSES1)]
-            if c >= PASSES1:
-                scale_features(c)
+            scaled = stages[(3, c + 1)] if c < DIRECT else h_tiles[c]
             result = results[c % len(results)]
             rows = out[c * P : (c + 1) * P, :] if c < PACK else out[K_PASS:H, :].rearrange("(p t) s -> p t s", t=PACK)[:, c - PACK, :]
             width = BANK // 2 if c == SLICES - 1 else BANK

@@ -21,16 +21,20 @@ P = 128
 PACK = 4
 K_PASS = P * PACK
 BANK = 512
+QUADRANT = 32
+LIST_ROWS = 16
 PASSES1 = K // K_PASS
 PASSES2 = H // K_PASS
 SLICES = H // P
-SLICES_PER_PASS = K_PASS // P
+LOW = K_PASS // P
 BLOCKS = R // P
-W1_CHUNKS = (128, 128, 256, 512)
-Y_WINDOW = R + 16
-TURN_LAG = 3
 HALF = R // 2
+W1_RANGES = (2 * P, 2 * P, K_PASS)
+FIRST, SECOND, HIGH = 0, 1, 2
+VECTOR_PIECE = (SECOND, 1)
+Y_WINDOW = R + LIST_ROWS
 DIRECT = 2
+ALIGN = 64
 
 
 def tile_list_graft_region_score_kernel(
@@ -44,156 +48,160 @@ def tile_list_graft_region_score_kernel(
         psum = ctx.enter_context(tc.psum_pool(name="psum", bufs=1))
         banks = [psum.tile([P, BANK], F32, name="bank%d" % i) for i in range(8)]
 
-        offs_sb = lists.tile([P, S // 16], U16, name="offs_sb")
-        pos1_sb = lists.tile([P, R // 16], U16, name="pos1_sb")
-        pos2_sb = lists.tile([P, R // 16], U16, name="pos2_sb")
-        pos3_sb = lists.tile([P, S // 16], U16, name="pos3_sb")
+        def held(shape, dtype, name, tag=None):
+            return keep.tile(shape, dtype, name=name, tag=tag or name, align_bytes=ALIGN)
 
-        tab_sc = keep.tile([P, T], U8, name="tab_sc", tag="shared", align_bytes=64)
-        w2_sc = keep.tile([P, PASSES2, H], U8, name="w2_sc", align_bytes=64)
-        w2_low = keep.tile([P, PASSES2, 2 * K_PASS], U8, name="w2_low", align_bytes=64)
-        w2_high = keep.tile([P, PASSES2, 2 * K_PASS], U8, name="w2_high", align_bytes=64)
-        w2_dealt = keep.tile([P, PASSES2, 2 * K_PASS], U8, name="w2_dealt", align_bytes=64)
-        w2_sc_dealt = keep.tile([P, PASSES2, K_PASS], U8, name="w2_sc_dealt", align_bytes=64)
-        high_cols = [keep.tile([P, PACK], F32, name="high_cols%d" % i, align_bytes=64) for i in range(3)]
-        tab_sb = [keep.tile([P, T], I32, name="tab_sb%d" % a, align_bytes=64) for a in range(PASSES1)]
-        v_words = [keep.tile([P, S], U32, name="v_words%d" % a, align_bytes=64) for a in range(PASSES1 - 1)]
-        v_sc = keep.tile([P, S], U8, name="v_sc", align_bytes=64)
-        y_tiles = [keep.tile([P, Y_WINDOW], F32, name="y%d" % i, align_bytes=64) for i in range(SLICES)]
-        ident = keep.tile([P, P], F32, name="ident", align_bytes=64)
-        vec_rows = keep.tile([P, P], F32, name="vec_rows", align_bytes=64)
-        vec_cols = keep.tile([P, 3 * PACK], F32, name="vec_cols", align_bytes=64)
+        offs_sb = lists.tile([P, S // LIST_ROWS], U16, name="offs_sb")
+        pos1_sb = lists.tile([P, R // LIST_ROWS], U16, name="pos1_sb")
+        pos2_sb = lists.tile([P, R // LIST_ROWS], U16, name="pos2_sb")
+        pos3_sb = lists.tile([P, S // LIST_ROWS], U16, name="pos3_sb")
 
-        sc_rows = keep.tile([P, T // 4], I32, name="sc_rows", align_bytes=64)
-        for q in range(4):
+        tab_sb = [held([P, T], I32, "tab_sb%d" % a) for a in range(PASSES1)]
+        tab_sc = held([P, T], U8, "tab_sc")
+        v_words = [held([P, S], U32, "v_words%d" % a) for a in range(PASSES1 - 1)]
+        v_sc = held([P, S], U8, "v_sc")
+        w2_sc = held([P, PASSES2, H], U8, "w2_sc")
+        w2_low = held([P, PASSES2, 2 * K_PASS], U8, "w2_low")
+        w2_high = held([P, PASSES2, 2 * K_PASS], U8, "w2_high")
+        y_tiles = [held([P, Y_WINDOW], F32, "y%d" % c) for c in range(SLICES)]
+        ident = held([P, P], F32, "ident")
+        bias_rows = held([P, P], F32, "bias_rows")
+        gain_rows = held([P, P], F32, "gain_rows")
+        low_gains = held([P, 2 * LOW], F32, "low_gains")
+        high_bias = held([P, PACK], F32, "high_bias")
+        high_gv = held([P, PACK], F32, "high_gv")
+        high_hv = held([P, PACK], F32, "high_hv")
+
+        nc.gpsimd.memset(tab_sc[:].bitcast(I32), 0)
+        for q in range(P // QUADRANT):
             nc.scalar.dma_start(
-                out=sc_rows[32 * q : 32 * q + 4 * PASSES1, :],
+                out=tab_sc[QUADRANT * q : QUADRANT * q + 4 * PASSES1, :].bitcast(I32),
                 in_=tab_scales[:, 4 * q : 4 * q + 4, :].bitcast(I32),
             )
-        nc.vector.memset(tab_sc[:].bitcast(I32), 0)
+        nc.vector.memset(bias_rows[:], 0.0)
         nc.vector.memset(w2_sc[:].rearrange("p a n -> p (a n)").bitcast(I32), 0)
         for y in y_tiles:
             nc.vector.memset(y[:, R:], 0.0)
-
-        nc.vector.memset(vec_rows[:], 0.0)
+        nc.vector.memset(gain_rows[:], 0.0)
         make_identity(nc, ident[:])
+
+        raws = {}
+
+        def raw_tag(piece):
+            return "raw%d_%d" % piece
+
+        def stage_tag(piece):
+            return "stage%d_%d" % piece
 
         def load_table(a):
             nc.sync.dma_start(out=tab_sb[a][:], in_=tab_words[a].rearrange("p t i -> p (t i)").bitcast(I32))
 
+        def load_piece(piece):
+            part, a = piece
+            c0, width = sum(W1_RANGES[:part]), W1_RANGES[part]
+            raws[piece] = held([P, PACK * width], F32, raw_tag(piece))
+            rows = w1[a * K_PASS : (a + 1) * K_PASS, c0 : c0 + width]
+            nc.sync.dma_start(
+                out=raws[piece][:].rearrange("p (j c) -> p j c", j=PACK), in_=rows.rearrange("(p j) c -> p j c", j=PACK)
+            )
+
+        def load_low_rows(rows, row0, vec):
+            nc.sync.dma_start(out=rows[row0 : row0 + LOW, :], in_=vec[0:K_PASS].rearrange("(c p) -> c p", p=P))
+
+        def load_high_columns(columns, vec):
+            nc.sync.dma_start(out=columns[:], in_=vec[K_PASS:H].rearrange("(p t) -> p t", t=PACK))
+
+        load_table(0)
+        nc.sync.dma_start(offs_sb[:], offs)
+        load_piece((FIRST, 0))
+        load_low_rows(bias_rows, 0, b1)
+        for a in range(1, PASSES1):
+            load_table(a)
+            load_piece((FIRST, a))
+        load_piece((SECOND, 0))
+        load_piece((SECOND, 1))
+        nc.sync.dma_start(pos1_sb[:], pos1)
+        nc.sync.dma_start(pos2_sb[:], pos2)
+        load_piece((SECOND, 2))
+        load_piece((HIGH, 0))
+        load_piece((HIGH, 1))
+        for q in range(P // QUADRANT):
+            nc.sync.dma_start(
+                out=w2_sc[QUADRANT * q : QUADRANT * q + 4, :, :].bitcast(I32),
+                in_=w2_scales[:, 4 * q : 4 * q + 4, :].bitcast(I32).rearrange("a r n -> r a n"),
+            )
+        load_piece((HIGH, 2))
+        load_high_columns(high_bias, b1)
+        w2_rows = w2_words.bitcast(I32).rearrange("a p n -> p a n")
+        nc.sync.dma_start(out=w2_high[:].bitcast(I32), in_=w2_rows[:, :, K_PASS // 2 : K_PASS])
+        load_low_rows(gain_rows, 0, gv)
+        load_low_rows(gain_rows, LOW, hv)
+        nc.sync.dma_start(out=w2_low[:].bitcast(I32), in_=w2_rows[:, :, 0 : K_PASS // 2])
+        load_high_columns(high_gv, gv)
+        load_high_columns(high_hv, hv)
+        nc.sync.dma_start(pos3_sb[:], pos3)
+
+        pieces = [(part, a) for part in range(len(W1_RANGES)) for a in range(PASSES1)]
+        alternating = [piece for piece in pieces if piece != VECTOR_PIECE][-(LOW + 1) :]
+        stages = {piece: held([P, 2 * W1_RANGES[piece[0]]], F32, stage_tag(piece)) for piece in pieces}
+
+        def bias_column(c):
+            return stages[alternating[c + 1]][:, 0:1] if c < LOW else high_bias[:, c - LOW : c - LOW + 1]
+
+        def gv_column(c):
+            return low_gains[:, c : c + 1] if c < LOW else high_gv[:, c - LOW : c - LOW + 1]
+
+        def hv_column(c):
+            return low_gains[:, LOW + c : LOW + c + 1] if c < LOW else high_hv[:, c - LOW : c - LOW + 1]
+
+        nc.tensor.transpose(banks[7][:, 0:P], bias_rows[:], ident[:])
+        for c in range(LOW):
+            nc.scalar.activation(out=bias_column(c), in_=banks[7][:, c : c + 1], func=ACT.Identity)
+
         def gather_table(a, lo, hi):
             nc.vector.tensor_copy(
-                out=v_words[a][:, lo:hi], in_=tab_sb[a][:].bitcast(U32).indirect(offs_sb[:, lo // 16 : hi // 16])
+                out=v_words[a][:, lo:hi],
+                in_=tab_sb[a][:].bitcast(U32).indirect(offs_sb[:, lo // LIST_ROWS : hi // LIST_ROWS]),
             )
+
+        gather_table(0, 0, S)
+        nc.vector.tensor_copy(out=v_sc[:], in_=tab_sc[:].indirect(offs_sb[:]))
+        gather_table(1, 0, S)
+        v_words.append(held([P, S], U32, "v_words2", tag="tab_sc"))
+        gather_table(2, 0, BANK)
+        gather_table(2, BANK, S)
 
         w1_codes = {}
         w1_scales = {}
-        stages = {}
 
-        def load_w1(chunk):
-            c0 = sum(W1_CHUNKS[:chunk])
-            width = W1_CHUNKS[chunk]
-            raws = []
-            for a in range(PASSES1):
-                raw = keep.tile([P, PACK * width], F32, name="raw%d_%d" % (chunk, a), tag="raw%d_%d" % (chunk, a), align_bytes=64)
-                rows = w1[a * K_PASS : (a + 1) * K_PASS, c0 : c0 + width]
-                nc.sync.dma_start(out=raw[:].rearrange("p (j c) -> p j c", j=PACK), in_=rows.rearrange("(p j) c -> p j c", j=PACK))
-                raws.append(raw)
-            return raws
-
-        def quantise_w1(chunk, raws):
-            c0 = sum(W1_CHUNKS[:chunk])
-            width = W1_CHUNKS[chunk]
-            for a in range(PASSES1):
-                stage = keep.tile([P, 2 * width], F32, name="stage%d_%d" % (chunk, a), align_bytes=64)
-                stages[(chunk, a)] = stage
-                grouped = stage[:].bitcast(BF16)
-                order = "p (i c j) -> p c j i" if width == K_PASS else "p (c i j) -> p c j i"
-                nc.scalar.copy(
-                    out=grouped.rearrange(order, i=4, j=PACK),
-                    in_=raws[a][:].rearrange("p (j c i) -> p c j i", i=4, j=PACK),
-                )
-                codes = keep.tile([P, width], U32, name="w1_codes%d_%d" % (chunk, a), align_bytes=64)
-                scales = keep.tile([P, width], U8, name="w1_scales%d_%d" % (chunk, a), align_bytes=64)
-                nc.vector.quantize_mx(
-                    out=codes[:].bitcast(FP8X4), scales=scales[:], in_=grouped
-                )
-                for off in range(0, width, P):
-                    w1_codes[((c0 + off) // P, a)] = codes[:, off : off + P]
-                    w1_scales[((c0 + off) // P, a)] = scales[:, off : off + P]
-
-        nc.sync.dma_start(offs_sb[:], offs)
-        load_table(0)
-        for i, vec in enumerate((b1, gv, hv)):
-            nc.sync.dma_start(
-                out=vec_rows[i * PACK : (i + 1) * PACK, :], in_=vec[0:K_PASS].rearrange("(c p) -> c p", p=P)
+        def quantise_piece(piece):
+            part, a = piece
+            c0, width = sum(W1_RANGES[:part]), W1_RANGES[part]
+            grouped = stages[piece][:].bitcast(BF16)
+            order = "p (i c j) -> p c j i" if part == HIGH else "p (c i j) -> p c j i"
+            copy = nc.vector.tensor_copy if piece == VECTOR_PIECE else nc.scalar.copy
+            copy(
+                out=grouped.rearrange(order, i=4, j=PACK),
+                in_=raws[piece][:].rearrange("p (j c i) -> p c j i", i=4, j=PACK),
             )
-        raws = {0: load_w1(0)}
-        load_table(1)
-        load_table(2)
-        w2_rows = w2_words.bitcast(I32).rearrange("a p n -> p a n")
-        nc.sync.dma_start(out=w2_high[:].bitcast(I32), in_=w2_rows[:, :, K_PASS // 2 : K_PASS])
-        for q in range(4):
-            nc.sync.dma_start(
-                out=w2_sc[32 * q : 32 * q + 4, :, :].bitcast(I32),
-                in_=w2_scales[:, 4 * q : 4 * q + 4, :].bitcast(I32).rearrange("a r n -> r a n"),
-            )
-        raws[1] = load_w1(1)
-        nc.sync.dma_start(pos1_sb[:], pos1)
-        nc.sync.dma_start(pos2_sb[:], pos2)
-        raws[2] = load_w1(2)
-        raws[3] = load_w1(3)
-        for i, vec in enumerate((b1, gv, hv)):
-            nc.sync.dma_start(out=high_cols[i][:], in_=vec[K_PASS:H].rearrange("(p t) -> p t", t=PACK))
-        nc.sync.dma_start(out=w2_low[:].bitcast(I32), in_=w2_rows[:, :, 0 : K_PASS // 2])
-        nc.sync.dma_start(pos3_sb[:], pos3)
+            codes = held([P, width], U32, "w1_codes%d_%d" % piece)
+            scales = held([P, width], U8, "w1_scales%d_%d" % piece)
+            nc.vector.quantize_mx(out=codes[:].bitcast(FP8X4), scales=scales[:], in_=grouped)
+            for off in range(0, width, P):
+                w1_codes[((c0 + off) // P, a)] = codes[:, off : off + P]
+                w1_scales[((c0 + off) // P, a)] = scales[:, off : off + P]
 
-        def column(i, c):
-            if c < PACK:
-                return vec_cols[:, i * PACK + c : i * PACK + c + 1]
-            return high_cols[i][:, c - PACK : c - PACK + 1]
-
-        for q in range(4):
-            rows = slice(32 * q, 32 * q + 4 * PASSES1)
-            nc.vector.tensor_copy(out=tab_sc[rows, :].bitcast(I32), in_=sc_rows[rows, :])
-        nc.tensor.transpose(banks[7][:, 0:P], vec_rows[:], ident[:])
-        nc.scalar.activation(out=vec_cols[:], in_=banks[7][:, 0 : 3 * PACK], func=ACT.Identity)
-        gather_table(0, 0, S)
-        nc.vector.tensor_copy(out=v_sc[:], in_=tab_sc[:].indirect(offs_sb[:]))
-        quantise_w1(0, raws[0])
-        gather_table(1, 0, S)
-        v_words.append(keep.tile([P, S], U32, name="v_words2", tag="shared", align_bytes=64))
-        gather_table(2, 0, BANK)
-        gather_table(2, BANK, S)
-        nc.vector.tensor_copy(
-            out=w2_dealt[:].bitcast(U16).rearrange("p a (t q) -> p a t q", t=PACK),
-            in_=w2_high[:].bitcast(U16).rearrange("p a (q t) -> p a t q", t=PACK),
-        )
-        nc.vector.tensor_copy(
-            out=w2_sc_dealt[:].rearrange("p a (t q) -> p a t q", t=PACK),
-            in_=w2_sc[:, :, K_PASS:H].rearrange("p a (q t) -> p a t q", t=PACK),
-        )
-        quantise_w1(1, raws[1])
-
-        spare = [keep.tile([P, R], F32, name="spare%d" % i, align_bytes=64) for i in range(2)]
         h_tiles = []
-        peaks = []
-        peak_codes = []
-        peak_scales = []
-        turned = keep.tile([P, BLOCKS, 2, 2 * P], BF16, name="turned", align_bytes=64)
-        for b in range(PASSES2):
-            peak_codes.append(keep.tile([P, R], U32, name="peak_codes%d" % b, align_bytes=64))
-            peak_scales.append(keep.tile([P, R], U8, name="peak_scales%d" % b, align_bytes=64))
-        for c in range(PACK):
-            peaks.append(keep.tile([P, R], F32, name="peak%d" % c, align_bytes=64)[:])
-        peak_high = keep.tile([P, PACK, R], F32, name="peak_high", align_bytes=64)
-        for t in range(PACK):
-            peaks.append(peak_high[:, t, :])
+        peak_codes = [held([P, R], U32, "peak_codes%d" % b) for b in range(PASSES2)]
+        peak_scales = [held([P, R], U8, "peak_scales%d" % b) for b in range(PASSES2)]
+        peak_high = held([P, PACK, R], F32, "peak_high")
+        peaks = [held([P, R], F32, "peak%d" % c)[:] for c in range(LOW)] + [peak_high[:, t, :] for t in range(PACK)]
+        low_grouped = held([P, 2 * R], F32, "low_grouped")
 
         def features(c):
-            tag = "raw3_%d" % (c - 1) if c in (2, 3) else "h%d" % c
-            h = keep.tile([P, S], F32, name="h%d" % c, tag=tag, align_bytes=64)
-            accs = banks[2 * (c % 2) : 2 * (c % 2) + 2]
+            h = held([P, S], F32, "h%d" % c, tag=raw_tag(alternating[c]) if c < LOW else None)
+            first_bank = 2 * (c % 2) if c < LOW else 2 * (c - LOW)
+            accs = banks[first_bank : first_bank + 2]
             for a in range(PASSES1):
                 for half in range(2):
                     cols = slice(half * BANK, (half + 1) * BANK)
@@ -211,30 +219,51 @@ def tile_list_graft_region_score_kernel(
                     out=h[:, half * BANK : (half + 1) * BANK],
                     in_=accs[half][:],
                     func=ACT.Identity,
-                    bias=column(0, c),
+                    bias=bias_column(c),
                     scale=1.0,
                 )
             h_tiles.append(h)
 
-        def pick(c, positions, dst, lo, hi):
-            nc.vector.tensor_copy(out=dst, in_=h_tiles[c][:].indirect(positions[:, lo // 16 : hi // 16]))
+        spare = [raws[VECTOR_PIECE][:, 0:R]] + [stages[(FIRST, a)][:] for a in range(PASSES1)]
+        picks = [
+            (spare[0], spare[1]),
+            (spare[2], spare[3]),
+            (spare[0], spare[1]),
+            (spare[2], stages[(HIGH, 2)][:, 0:R]),
+            (stages[(HIGH, 0)][:, 0:R], stages[(HIGH, 0)][:, R : 2 * R]),
+            (stages[(SECOND, 0)][:], stages[(SECOND, 1)][:]),
+            (stages[(SECOND, 2)][:], spare[3]),
+            (low_grouped[:, 0:R], low_grouped[:, R : 2 * R]),
+        ]
 
-        def staging(c):
-            if c in (0, 4):
-                return spare[0][:], spare[1][:]
-            if c == 1:
-                return stages[(2, 2)][:], stages[(2, 1)][:]
-            stage = stages[(3, {2: 0, 3: 2, 5: 1, 6: 2, 7: 0}[c])]
-            return stage[:, 0:R], stage[:, R : 2 * R]
+        def pick(c, positions, dst, lo, hi):
+            nc.vector.tensor_copy(out=dst, in_=h_tiles[c][:].indirect(positions[:, lo // LIST_ROWS : hi // LIST_ROWS]))
 
         def maxima(c):
-            first, second = staging(c)
+            first, second = picks[c]
             halves = (slice(0, HALF), slice(HALF, R))
             pick(c, pos1_sb, first, 0, R)
             for cols in halves:
                 pick(c, pos2_sb, second[:, cols], cols.start, cols.stop)
             for cols in halves:
                 nc.vector.tensor_tensor(out=peaks[c][:, cols], in0=first[:, cols], in1=second[:, cols], op=ALU.max)
+
+        for piece in pieces[: pieces.index(VECTOR_PIECE) + 1]:
+            quantise_piece(piece)
+        for c in range(LOW - 1):
+            features(c)
+            maxima(c)
+            quantise_piece(alternating[c + 1])
+        features(LOW - 1)
+        w2_sc_dealt = held([P, PASSES2, K_PASS], U8, "w2_sc_dealt", tag=stage_tag(alternating[LOW - 1]))
+        nc.vector.tensor_copy(
+            out=w2_sc_dealt[:].rearrange("p a (t q) -> p a t q", t=PACK),
+            in_=w2_sc[:, :, K_PASS:H].rearrange("p a (q t) -> p a t q", t=PACK),
+        )
+        quantise_piece(alternating[LOW])
+        maxima(LOW - 1)
+
+        turned = held([P, BLOCKS, 2, 2 * P], BF16, "turned", tag=raw_tag(alternating[LOW]))
 
         def turn(c, bank):
             for j in range(BLOCKS):
@@ -244,81 +273,82 @@ def tile_list_graft_region_score_kernel(
                 in_=bank[:].rearrange("p (j q u e) -> p u j q e", j=BLOCKS, u=2, e=2),
             )
 
-        def quantise_low_peak():
+        def group_low_peaks():
             words = turned[:].bitcast(F32)
-            grouped = keep.tile([P, R * PACK], BF16, name="low_grouped", align_bytes=64)
-            grouped_words = grouped[:].bitcast(F32).rearrange("p (j m u) -> p j m u", m=P, u=2)
+            grouped_words = low_grouped[:].rearrange("p (j m u) -> p j m u", m=P, u=2)
             for j0 in range(0, BLOCKS, 2):
-                bank = banks[4 + j0 // 2][:].rearrange("p (j u m) -> p j u m", u=2, m=P)
+                bank = banks[2 + j0 // 2][:].rearrange("p (j u m) -> p j u m", u=2, m=P)
                 for j in range(2):
                     for u in range(2):
                         nc.tensor.transpose(bank[:, j, u, :], words[:, j0 + j, u, :], ident[:])
                 nc.scalar.copy(out=grouped_words[:, j0 : j0 + 2, :, :], in_=bank.rearrange("p j u m -> p j m u"))
-            nc.vector.quantize_mx(out=peak_codes[0][:].bitcast(FP8X4), scales=peak_scales[0][:], in_=grouped[:])
 
-        def quantise_high_peak():
-            grouped = [
-                keep.tile([P, HALF * PACK], BF16, name="high_grouped%d" % i, align_bytes=64) for i in range(2)
-            ]
-            for i, copy in enumerate((nc.scalar.copy, nc.vector.tensor_copy)):
-                copy(
-                    out=grouped[i][:].rearrange("p (c i t) -> p c t i", i=4, t=PACK),
-                    in_=peak_high[:, :, i * HALF : (i + 1) * HALF].rearrange("p t (c i) -> p c t i", i=4),
-                )
-            for i in (1, 0):
-                cols = slice(i * HALF, (i + 1) * HALF)
-                nc.vector.quantize_mx(
-                    out=peak_codes[1][:, cols].bitcast(FP8X4), scales=peak_scales[1][:, cols], in_=grouped[i][:]
-                )
+        features(LOW)
+        nc.tensor.transpose(banks[7][:, 0:P], gain_rows[:], ident[:])
+        nc.scalar.copy(out=low_gains[:], in_=banks[7][:, 0 : 2 * LOW])
+        gv_hv = held([P, DIRECT], F32, "gv_hv")
+        nc.vector.tensor_tensor(out=gv_hv[:], in0=low_gains[:, 0:DIRECT], in1=low_gains[:, LOW : LOW + DIRECT], op=ALU.mult)
+        turn(0, banks[4])
+        turn(1, banks[5])
+        for c in range(LOW + 1, SLICES):
+            features(c)
+        turn(2, banks[0])
+        turn(3, banks[1])
+        group_low_peaks()
 
-        def scale_features(c):
-            nc.scalar.activation(
-                out=stages[(3, (c + 1) % PASSES1)][:],
-                in_=h_tiles[c][:],
-                func=ACT.Copy,
-                scale=column(2, c),
+        weighted = []
+
+        def weigh(c, dst):
+            scale = gv_hv[:, c : c + 1] if c < DIRECT else gv_column(c)
+            nc.scalar.activation(out=dst, in_=peaks[c], func=ACT.Copy, scale=scale)
+            weighted.append(dst)
+
+        for c in range(LOW, SLICES - 1):
+            maxima(c)
+            for dst in picks[c]:
+                weigh(len(weighted), dst)
+        nc.vector.quantize_mx(out=peak_codes[0][:].bitcast(FP8X4), scales=peak_scales[0][:], in_=low_grouped[:].bitcast(BF16))
+        maxima(SLICES - 1)
+
+        high_grouped = [held([P, HALF * PACK], BF16, "high_grouped%d" % i) for i in range(2)]
+        for i, copy in enumerate((nc.scalar.copy, nc.vector.tensor_copy)):
+            copy(
+                out=high_grouped[i][:].rearrange("p (c i t) -> p c t i", i=4, t=PACK),
+                in_=peak_high[:, :, i * HALF : (i + 1) * HALF].rearrange("p t (c i) -> p c t i", i=4),
             )
-
-        for step in range(SLICES):
-            features(step)
-            if step < 2:
-                quantise_w1(2 + step, raws[2 + step])
-            maxima(step)
-            c = step - TURN_LAG
-            if 0 <= c < PACK:
-                turn(c, banks[2 * (step % 2)])
-            if c == PACK - 1:
-                quantise_low_peak()
-        quantise_high_peak()
-        for c in range(DIRECT):
-            scale_features(c)
-        weighted_tiles = [tile[:] for tile in spare] + [stages[(2, a)][:] for a in range(PASSES1)]
-        weighted_tiles.append(stages[(3, 0)][:, 0:R])
+        for i in (1, 0):
+            cols = slice(i * HALF, (i + 1) * HALF)
+            nc.vector.quantize_mx(
+                out=peak_codes[1][:, cols].bitcast(FP8X4), scales=peak_scales[1][:, cols], in_=high_grouped[i][:]
+            )
+        w2_dealt = held([P, PASSES2, 2 * K_PASS], U8, "w2_dealt", tag="high_grouped0")
+        nc.vector.tensor_copy(
+            out=w2_dealt[:].bitcast(U16).rearrange("p a (t q) -> p a t q", t=PACK),
+            in_=w2_high[:].bitcast(U16).rearrange("p a (q t) -> p a t q", t=PACK),
+        )
 
         def add_by_transposes(c, bounded):
-            weighted = weighted_tiles[c - DIRECT]
-            nc.scalar.activation(out=weighted, in_=peaks[c], func=ACT.Copy, scale=column(1, c))
             sums = banks[c % 2]
             back = banks[2 + c % 2]
             for j in range(BLOCKS):
                 cols = slice(j * P, (j + 1) * P)
                 nc.tensor.matmul(
-                    out=sums[:, cols], lhsT=weighted[:, cols], rhs=ident[:], is_transpose=True, start=True, stop=False
+                    out=sums[:, cols], lhsT=weighted[c][:, cols], rhs=ident[:], is_transpose=True, start=True, stop=False
                 )
                 nc.tensor.matmul(
                     out=sums[:, cols], lhsT=bounded[:, cols], rhs=ident[:], is_transpose=True, start=False, stop=True
                 )
-            summed = ring.tile([P, R], F32, name="summed", tag="summed", align_bytes=64)
+            summed = ring.tile([P, R], F32, name="summed", tag="summed", align_bytes=ALIGN)
             nc.scalar.copy(out=summed[:], in_=sums[:])
             for j in range(BLOCKS):
                 cols = slice(j * P, (j + 1) * P)
                 nc.tensor.transpose(back[:, cols], summed[:, cols], ident[:])
-            nc.scalar.activation(out=y_tiles[c][:, 0:R], in_=back[:], func=ACT.Copy, scale=column(2, c))
+            nc.scalar.activation(out=y_tiles[c][:, 0:R], in_=back[:], func=ACT.Copy, scale=hv_column(c))
 
         def scores(c):
             acc = banks[4 + (c + 2) % 4]
-            words, scales = (w2_low, w2_sc) if c < PACK else (w2_dealt, w2_sc_dealt)
-            n = c % PACK
+            words, scales = (w2_low, w2_sc) if c < LOW else (w2_dealt, w2_sc_dealt)
+            n = c % LOW
             for b in range(PASSES2):
                 nc.tensor.matmul_mx(
                     out=acc[:],
@@ -329,41 +359,44 @@ def tile_list_graft_region_score_kernel(
                     start=(b == 0),
                     stop=(b == PASSES2 - 1),
                 )
-            bounded = ring.tile([P, R], F32, name="bounded", tag="bounded", bufs=3, align_bytes=64)
+            bounded = ring.tile([P, R], F32, name="bounded", tag="bounded", bufs=3, align_bytes=ALIGN)
             if c >= DIRECT:
                 nc.scalar.activation(out=bounded[:], in_=acc[:], func=ACT.Tanh)
+                if c == len(weighted):
+                    weigh(c, weighted[c % DIRECT])
                 add_by_transposes(c, bounded)
                 return
-            width = R // 2 if c == 0 else R
+            width = HALF if c == 0 else R
             for lo in range(0, R, width):
                 cols = slice(lo, lo + width)
                 nc.scalar.activation(out=bounded[:, cols], in_=acc[:, cols], func=ACT.Tanh)
                 nc.vector.scalar_tensor_tensor(
                     out=y_tiles[c][:, cols],
-                    in0=peaks[c][:, cols],
-                    scalar=column(1, c),
-                    in1=bounded[:, cols],
+                    in0=bounded[:, cols],
+                    scalar=hv_column(c),
+                    in1=weighted[c][:, cols],
                     op0=ALU.mult,
                     op1=ALU.add,
                 )
 
-        results = [raw[:] for raw in raws[2]] + [raws[3][0][:, 0:S], raws[3][0][:, S : 2 * S]]
+        results = [raws[piece][:] for piece in pieces if piece not in alternating]
+        high_rows = out[K_PASS:H, :].rearrange("(p t) s -> p t s", t=PACK)
 
         def finish(c):
-            scaled = stages[(3, c + 1)] if c < DIRECT else h_tiles[c]
+            last = c == SLICES - 1
             result = results[c % len(results)]
-            rows = out[c * P : (c + 1) * P, :] if c < PACK else out[K_PASS:H, :].rearrange("(p t) s -> p t s", t=PACK)[:, c - PACK, :]
-            width = BANK // 2 if c == SLICES - 1 else BANK
+            rows = out[c * P : (c + 1) * P, :] if c < LOW else high_rows[:, c - LOW, :]
+            width = HALF if last else R
             for lo in range(0, S, width):
                 nc.vector.tensor_tensor(
                     out=result[:, lo : lo + width],
-                    in0=y_tiles[c][:].indirect(pos3_sb[:, lo // 16 : (lo + width) // 16]),
-                    in1=scaled[:, lo : lo + width],
+                    in0=y_tiles[c][:].indirect(pos3_sb[:, lo // LIST_ROWS : (lo + width) // LIST_ROWS]),
+                    in1=h_tiles[c][:, lo : lo + width],
                     op=ALU.mult,
                 )
-                if c == SLICES - 1:
+                if last:
                     nc.sync.dma_start(out=rows[:, lo : lo + width], in_=result[:, lo : lo + width])
-            if c < SLICES - 1:
+            if not last:
                 nc.sync.dma_start(out=rows, in_=result)
 
         scores(0)

from contextlib import ExitStack

import concourse.mybir as mybir
from concourse.masks import make_identity

K, H, T, S, R = 1536, 1024, 2048, 1024, 512
FLOPS = 2 * K * H * S + 2 * H * H * R

F32 = mybir.dt.float32
BF16 = mybir.dt.bfloat16
I32 = mybir.dt.int32
U32 = mybir.dt.uint32
U16 = mybir.dt.uint16
U8 = mybir.dt.uint8
FP8X4 = mybir.dt.float8_e4m3fn_x4
FP4X4 = mybir.dt.float4_e2m1fn_x4
ALU = mybir.AluOpType
ACT = mybir.ActivationFunctionType

P = 128
PACK = 4
K_PASS = P * PACK
BANK = 512
QUADRANT = 32
LIST_ROWS = 16
PASSES1 = K // K_PASS
PASSES2 = H // K_PASS
SLICES = H // P
LOW = K_PASS // P
BLOCKS = R // P
HALF = R // 2
W1_RANGES = (2 * P, 2 * P, K_PASS)
FIRST, SECOND, HIGH = 0, 1, 2
VECTOR_PIECE = (SECOND, 1)
Y_WINDOW = R + LIST_ROWS
DIRECT = 2
ALIGN = 64


def tile_list_graft_region_score_kernel(
    tc, tab_words, tab_scales, offs, w1, b1, pos1, pos2, pos3, w2_words, w2_scales, gv, hv, out
):
    nc = tc.nc
    with ExitStack() as ctx:
        lists = ctx.enter_context(tc.tile_pool(name="lists", bufs=1))
        keep = ctx.enter_context(tc.tile_pool(name="keep", bufs=1))
        ring = ctx.enter_context(tc.tile_pool(name="ring", bufs=2))
        psum = ctx.enter_context(tc.psum_pool(name="psum", bufs=1))
        banks = [psum.tile([P, BANK], F32, name="bank%d" % i) for i in range(8)]

        def held(shape, dtype, name, tag=None):
            return keep.tile(shape, dtype, name=name, tag=tag or name, align_bytes=ALIGN)

        offs_sb = lists.tile([P, S // LIST_ROWS], U16, name="offs_sb")
        pos1_sb = lists.tile([P, R // LIST_ROWS], U16, name="pos1_sb")
        pos2_sb = lists.tile([P, R // LIST_ROWS], U16, name="pos2_sb")
        pos3_sb = lists.tile([P, S // LIST_ROWS], U16, name="pos3_sb")

        tab_sb = [held([P, T], I32, "tab_sb%d" % a) for a in range(PASSES1)]
        tab_sc = held([P, T], U8, "tab_sc")
        v_words = [held([P, S], U32, "v_words%d" % a) for a in range(PASSES1 - 1)]
        v_sc = held([P, S], U8, "v_sc")
        w2_sc = held([P, PASSES2, H], U8, "w2_sc")
        w2_low = held([P, PASSES2, 2 * K_PASS], U8, "w2_low")
        w2_high = held([P, PASSES2, 2 * K_PASS], U8, "w2_high")
        y_tiles = [held([P, Y_WINDOW], F32, "y%d" % c) for c in range(SLICES)]
        ident = held([P, P], F32, "ident")
        bias_rows = held([P, P], F32, "bias_rows")
        gain_rows = held([P, P], F32, "gain_rows")
        low_gains = held([P, 2 * LOW], F32, "low_gains")
        high_bias = held([P, PACK], F32, "high_bias")
        high_gv = held([P, PACK], F32, "high_gv")
        high_hv = held([P, PACK], F32, "high_hv")

        nc.gpsimd.memset(tab_sc[:].bitcast(I32), 0)
        for q in range(P // QUADRANT):
            nc.scalar.dma_start(
                out=tab_sc[QUADRANT * q : QUADRANT * q + 4 * PASSES1, :].bitcast(I32),
                in_=tab_scales[:, 4 * q : 4 * q + 4, :].bitcast(I32),
            )
        nc.vector.memset(bias_rows[:], 0.0)
        nc.vector.memset(w2_sc[:].rearrange("p a n -> p (a n)").bitcast(I32), 0)
        for y in y_tiles:
            nc.vector.memset(y[:, R:], 0.0)
        nc.vector.memset(gain_rows[:], 0.0)
        make_identity(nc, ident[:])

        raws = {}

        def raw_tag(piece):
            return "raw%d_%d" % piece

        def stage_tag(piece):
            return "stage%d_%d" % piece

        def load_table(a):
            nc.sync.dma_start(out=tab_sb[a][:], in_=tab_words[a].rearrange("p t i -> p (t i)").bitcast(I32))

        def load_piece(piece):
            part, a = piece
            c0, width = sum(W1_RANGES[:part]), W1_RANGES[part]
            raws[piece] = held([P, PACK * width], F32, raw_tag(piece))
            rows = w1[a * K_PASS : (a + 1) * K_PASS, c0 : c0 + width]
            nc.sync.dma_start(
                out=raws[piece][:].rearrange("p (j c) -> p j c", j=PACK), in_=rows.rearrange("(p j) c -> p j c", j=PACK)
            )

        def load_low_rows(rows, row0, vec):
            nc.sync.dma_start(out=rows[row0 : row0 + LOW, :], in_=vec[0:K_PASS].rearrange("(c p) -> c p", p=P))

        def load_high_columns(columns, vec):
            nc.sync.dma_start(out=columns[:], in_=vec[K_PASS:H].rearrange("(p t) -> p t", t=PACK))

        load_table(0)
        nc.sync.dma_start(offs_sb[:], offs)
        load_piece((FIRST, 0))
        load_low_rows(bias_rows, 0, b1)
        for a in range(1, PASSES1):
            load_table(a)
            load_piece((FIRST, a))
        load_piece((SECOND, 0))
        load_piece((SECOND, 1))
        nc.sync.dma_start(pos1_sb[:], pos1)
        nc.sync.dma_start(pos2_sb[:], pos2)
        load_piece((SECOND, 2))
        load_piece((HIGH, 0))
        load_piece((HIGH, 1))
        for q in range(P // QUADRANT):
            nc.sync.dma_start(
                out=w2_sc[QUADRANT * q : QUADRANT * q + 4, :, :].bitcast(I32),
                in_=w2_scales[:, 4 * q : 4 * q + 4, :].bitcast(I32).rearrange("a r n -> r a n"),
            )
        load_piece((HIGH, 2))
        load_high_columns(high_bias, b1)
        w2_rows = w2_words.bitcast(I32).rearrange("a p n -> p a n")
        nc.sync.dma_start(out=w2_high[:].bitcast(I32), in_=w2_rows[:, :, K_PASS // 2 : K_PASS])
        load_low_rows(gain_rows, 0, gv)
        load_low_rows(gain_rows, LOW, hv)
        nc.sync.dma_start(out=w2_low[:].bitcast(I32), in_=w2_rows[:, :, 0 : K_PASS // 2])
        load_high_columns(high_gv, gv)
        load_high_columns(high_hv, hv)
        nc.sync.dma_start(pos3_sb[:], pos3)

        pieces = [(part, a) for part in range(len(W1_RANGES)) for a in range(PASSES1)]
        alternating = [piece for piece in pieces if piece != VECTOR_PIECE][-(LOW + 1) :]
        stages = {piece: held([P, 2 * W1_RANGES[piece[0]]], F32, stage_tag(piece)) for piece in pieces}

        def bias_column(c):
            return stages[alternating[c + 1]][:, 0:1] if c < LOW else high_bias[:, c - LOW : c - LOW + 1]

        def gv_column(c):
            return low_gains[:, c : c + 1] if c < LOW else high_gv[:, c - LOW : c - LOW + 1]

        def hv_column(c):
            return low_gains[:, LOW + c : LOW + c + 1] if c < LOW else high_hv[:, c - LOW : c - LOW + 1]

        nc.tensor.transpose(banks[7][:, 0:P], bias_rows[:], ident[:])
        for c in range(LOW):
            nc.scalar.activation(out=bias_column(c), in_=banks[7][:, c : c + 1], func=ACT.Identity)

        def gather_table(a, lo, hi):
            nc.vector.tensor_copy(
                out=v_words[a][:, lo:hi],
                in_=tab_sb[a][:].bitcast(U32).indirect(offs_sb[:, lo // LIST_ROWS : hi // LIST_ROWS]),
            )

        gather_table(0, 0, S)
        nc.vector.tensor_copy(out=v_sc[:], in_=tab_sc[:].indirect(offs_sb[:]))
        gather_table(1, 0, S)
        v_words.append(held([P, S], U32, "v_words2", tag="tab_sc"))
        gather_table(2, 0, BANK)
        gather_table(2, BANK, S)

        w1_codes = {}
        w1_scales = {}

        def quantise_piece(piece):
            part, a = piece
            c0, width = sum(W1_RANGES[:part]), W1_RANGES[part]
            grouped = stages[piece][:].bitcast(BF16)
            order = "p (i c j) -> p c j i" if part == HIGH else "p (c i j) -> p c j i"
            copy = nc.vector.tensor_copy if piece == VECTOR_PIECE else nc.scalar.copy
            copy(
                out=grouped.rearrange(order, i=4, j=PACK),
                in_=raws[piece][:].rearrange("p (j c i) -> p c j i", i=4, j=PACK),
            )
            codes = held([P, width], U32, "w1_codes%d_%d" % piece)
            scales = held([P, width], U8, "w1_scales%d_%d" % piece)
            nc.vector.quantize_mx(out=codes[:].bitcast(FP8X4), scales=scales[:], in_=grouped)
            for off in range(0, width, P):
                w1_codes[((c0 + off) // P, a)] = codes[:, off : off + P]
                w1_scales[((c0 + off) // P, a)] = scales[:, off : off + P]

        h_tiles = []
        peak_codes = [held([P, R], U32, "peak_codes%d" % b) for b in range(PASSES2)]
        peak_scales = [held([P, R], U8, "peak_scales%d" % b) for b in range(PASSES2)]
        peak_high = held([P, PACK, R], F32, "peak_high")
        peaks = [held([P, R], F32, "peak%d" % c)[:] for c in range(LOW)] + [peak_high[:, t, :] for t in range(PACK)]
        low_grouped = held([P, 2 * R], F32, "low_grouped")

        def features(c):
            h = held([P, S], F32, "h%d" % c, tag=raw_tag(alternating[c]) if c < LOW else None)
            first_bank = 2 * (c % 2) if c < LOW else 2 * (c - LOW)
            accs = banks[first_bank : first_bank + 2]
            for a in range(PASSES1):
                for half in range(2):
                    cols = slice(half * BANK, (half + 1) * BANK)
                    nc.tensor.matmul_mx(
                        out=accs[half][:],
                        lhsT=w1_codes[(c, a)].bitcast(FP8X4),
                        lhsT_scale=w1_scales[(c, a)],
                        rhs=v_words[a][:, cols].bitcast(FP8X4),
                        rhs_scale=v_sc[4 * a : P, cols],
                        start=(a == 0),
                        stop=(a == PASSES1 - 1),
                    )
            for half in range(2):
                nc.scalar.activation(
                    out=h[:, half * BANK : (half + 1) * BANK],
                    in_=accs[half][:],
                    func=ACT.Identity,
                    bias=bias_column(c),
                    scale=1.0,
                )
            h_tiles.append(h)

        spare = [raws[VECTOR_PIECE][:, 0:R]] + [stages[(FIRST, a)][:] for a in range(PASSES1)]
        picks = [
            (spare[0], spare[1]),
            (spare[2], spare[3]),
            (spare[0], spare[1]),
            (spare[2], stages[(HIGH, 2)][:, 0:R]),
            (stages[(HIGH, 0)][:, 0:R], stages[(HIGH, 0)][:, R : 2 * R]),
            (stages[(SECOND, 0)][:], stages[(SECOND, 1)][:]),
            (stages[(SECOND, 2)][:], spare[3]),
            (low_grouped[:, 0:R], low_grouped[:, R : 2 * R]),
        ]

        def pick(c, positions, dst, lo, hi):
            nc.vector.tensor_copy(out=dst, in_=h_tiles[c][:].indirect(positions[:, lo // LIST_ROWS : hi // LIST_ROWS]))

        def maxima(c):
            first, second = picks[c]
            halves = (slice(0, HALF), slice(HALF, R))
            pick(c, pos1_sb, first, 0, R)
            for cols in halves:
                pick(c, pos2_sb, second[:, cols], cols.start, cols.stop)
            for cols in halves:
                nc.vector.tensor_tensor(out=peaks[c][:, cols], in0=first[:, cols], in1=second[:, cols], op=ALU.max)

        for piece in pieces[: pieces.index(VECTOR_PIECE) + 1]:
            quantise_piece(piece)
        for c in range(LOW - 1):
            features(c)
            maxima(c)
            quantise_piece(alternating[c + 1])
        features(LOW - 1)
        w2_sc_dealt = held([P, PASSES2, K_PASS], U8, "w2_sc_dealt", tag=stage_tag(alternating[LOW - 1]))
        nc.vector.tensor_copy(
            out=w2_sc_dealt[:].rearrange("p a (t q) -> p a t q", t=PACK),
            in_=w2_sc[:, :, K_PASS:H].rearrange("p a (q t) -> p a t q", t=PACK),
        )
        quantise_piece(alternating[LOW])
        maxima(LOW - 1)

        turned = held([P, BLOCKS, 2, 2 * P], BF16, "turned", tag=raw_tag(alternating[LOW]))

        def turn(c, bank):
            for j in range(BLOCKS):
                nc.tensor.transpose(bank[:, j * P : (j + 1) * P], peaks[c][:, j * P : (j + 1) * P], ident[:])
            nc.scalar.copy(
                out=turned[:, :, :, 64 * c : 64 * (c + 1)].rearrange("p j u (q e) -> p u j q e", e=2),
                in_=bank[:].rearrange("p (j q u e) -> p u j q e", j=BLOCKS, u=2, e=2),
            )

        def group_low_peaks():
            words = turned[:].bitcast(F32)
            grouped_words = low_grouped[:].rearrange("p (j m u) -> p j m u", m=P, u=2)
            for j0 in range(0, BLOCKS, 2):
                bank = banks[2 + j0 // 2][:].rearrange("p (j u m) -> p j u m", u=2, m=P)
                for j in range(2):
                    for u in range(2):
                        nc.tensor.transpose(bank[:, j, u, :], words[:, j0 + j, u, :], ident[:])
                nc.scalar.copy(out=grouped_words[:, j0 : j0 + 2, :, :], in_=bank.rearrange("p j u m -> p j m u"))

        features(LOW)
        nc.tensor.transpose(banks[7][:, 0:P], gain_rows[:], ident[:])
        nc.scalar.copy(out=low_gains[:], in_=banks[7][:, 0 : 2 * LOW])
        gv_hv = held([P, DIRECT], F32, "gv_hv")
        nc.vector.tensor_tensor(out=gv_hv[:], in0=low_gains[:, 0:DIRECT], in1=low_gains[:, LOW : LOW + DIRECT], op=ALU.mult)
        turn(0, banks[4])
        turn(1, banks[5])
        for c in range(LOW + 1, SLICES):
            features(c)
        turn(2, banks[0])
        turn(3, banks[1])
        group_low_peaks()

        weighted = []

        def weigh(c, dst):
            scale = gv_hv[:, c : c + 1] if c < DIRECT else gv_column(c)
            nc.scalar.activation(out=dst, in_=peaks[c], func=ACT.Copy, scale=scale)
            weighted.append(dst)

        for c in range(LOW, SLICES - 1):
            maxima(c)
            for dst in picks[c]:
                weigh(len(weighted), dst)
        nc.vector.quantize_mx(out=peak_codes[0][:].bitcast(FP8X4), scales=peak_scales[0][:], in_=low_grouped[:].bitcast(BF16))
        maxima(SLICES - 1)

        high_grouped = [held([P, HALF * PACK], BF16, "high_grouped%d" % i) for i in range(2)]
        for i, copy in enumerate((nc.scalar.copy, nc.vector.tensor_copy)):
            copy(
                out=high_grouped[i][:].rearrange("p (c i t) -> p c t i", i=4, t=PACK),
                in_=peak_high[:, :, i * HALF : (i + 1) * HALF].rearrange("p t (c i) -> p c t i", i=4),
            )
        for i in (1, 0):
            cols = slice(i * HALF, (i + 1) * HALF)
            nc.vector.quantize_mx(
                out=peak_codes[1][:, cols].bitcast(FP8X4), scales=peak_scales[1][:, cols], in_=high_grouped[i][:]
            )
        w2_dealt = held([P, PASSES2, 2 * K_PASS], U8, "w2_dealt", tag="high_grouped0")
        nc.vector.tensor_copy(
            out=w2_dealt[:].bitcast(U16).rearrange("p a (t q) -> p a t q", t=PACK),
            in_=w2_high[:].bitcast(U16).rearrange("p a (q t) -> p a t q", t=PACK),
        )

        def add_by_transposes(c, bounded):
            sums = banks[c % 2]
            back = banks[2 + c % 2]
            for j in range(BLOCKS):
                cols = slice(j * P, (j + 1) * P)
                nc.tensor.matmul(
                    out=sums[:, cols], lhsT=weighted[c][:, cols], rhs=ident[:], is_transpose=True, start=True, stop=False
                )
                nc.tensor.matmul(
                    out=sums[:, cols], lhsT=bounded[:, cols], rhs=ident[:], is_transpose=True, start=False, stop=True
                )
            summed = ring.tile([P, R], F32, name="summed", tag="summed", align_bytes=ALIGN)
            nc.scalar.copy(out=summed[:], in_=sums[:])
            for j in range(BLOCKS):
                cols = slice(j * P, (j + 1) * P)
                nc.tensor.transpose(back[:, cols], summed[:, cols], ident[:])
            nc.scalar.activation(out=y_tiles[c][:, 0:R], in_=back[:], func=ACT.Copy, scale=hv_column(c))

        def scores(c):
            acc = banks[4 + (c + 2) % 4]
            words, scales = (w2_low, w2_sc) if c < LOW else (w2_dealt, w2_sc_dealt)
            n = c % LOW
            for b in range(PASSES2):
                nc.tensor.matmul_mx(
                    out=acc[:],
                    lhsT=words[:, b, 2 * P * n : 2 * P * (n + 1)].bitcast(FP4X4),
                    lhsT_scale=scales[:, b, P * n : P * (n + 1)],
                    rhs=peak_codes[b][:].bitcast(FP8X4),
                    rhs_scale=peak_scales[b][:],
                    start=(b == 0),
                    stop=(b == PASSES2 - 1),
                )
            bounded = ring.tile([P, R], F32, name="bounded", tag="bounded", bufs=3, align_bytes=ALIGN)
            if c >= DIRECT:
                nc.scalar.activation(out=bounded[:], in_=acc[:], func=ACT.Tanh)
                if c == len(weighted):
                    weigh(c, weighted[c % DIRECT])
                add_by_transposes(c, bounded)
                return
            width = HALF if c == 0 else R
            for lo in range(0, R, width):
                cols = slice(lo, lo + width)
                nc.scalar.activation(out=bounded[:, cols], in_=acc[:, cols], func=ACT.Tanh)
                nc.vector.scalar_tensor_tensor(
                    out=y_tiles[c][:, cols],
                    in0=bounded[:, cols],
                    scalar=hv_column(c),
                    in1=weighted[c][:, cols],
                    op0=ALU.mult,
                    op1=ALU.add,
                )

        results = [raws[piece][:] for piece in pieces if piece not in alternating]
        high_rows = out[K_PASS:H, :].rearrange("(p t) s -> p t s", t=PACK)

        def finish(c):
            last = c == SLICES - 1
            result = results[c % len(results)]
            rows = out[c * P : (c + 1) * P, :] if c < LOW else high_rows[:, c - LOW, :]
            width = HALF if last else R
            for lo in range(0, S, width):
                nc.vector.tensor_tensor(
                    out=result[:, lo : lo + width],
                    in0=y_tiles[c][:].indirect(pos3_sb[:, lo // LIST_ROWS : (lo + width) // LIST_ROWS]),
                    in1=h_tiles[c][:, lo : lo + width],
                    op=ALU.mult,
                )
                if last:
                    nc.sync.dma_start(out=rows[:, lo : lo + width], in_=result[:, lo : lo + width])
            if not last:
                nc.sync.dma_start(out=rows, in_=result)

        scores(0)
        for c in range(SLICES):
            if c + 1 < SLICES:
                scores(c + 1)
            finish(c)
